import numpy as np
CORES = [65,66,69,71,193,194,197,199,321,322,325,327,449,450,453,455]
N = 16
R, W, T = 8192, 64, 1024
CAPP = 256
def entries(a): return a.T.reshape(-1)
def pack(v, P): return np.ascontiguousarray(np.asarray(v, np.int32).reshape(-1, P).T)
def lists(rng, how):
    I = rng.integers(0, N * R, (N, T))
    O = np.stack([rng.permutation(np.repeat(np.arange(N), CAPP))[:T] for r in range(N)])
    if how == "full": O = np.stack([rng.permutation(np.repeat(rng.permutation(N)[:T // CAPP], CAPP)) for r in range(N)])
    I = R * O + rng.integers(0, R, (N, T))
    if how == "alike": I = R * O + rng.integers(0, R, (N, 1))
    if how == "edge": I = R * O + np.where(rng.random((N, T)) < 0.5, 0, R - 1)
    if how == "sorted": I = np.sort(I, axis=1)
    return {"idx": np.stack([pack(I[r], 128) for r in range(N)])}
def setup_inputs(rng):
    return dict({"tab": rng.standard_normal((N, R, W), dtype=np.float32)}, **lists(rng, "uniform"))
def setup_inputs_alike(rng):
    d = setup_inputs(rng); d.update(lists(rng, "alike"))
    for k in ("tab",): d[k] = (d[k].astype(np.float32) * 1048576.0).astype(d[k].dtype)
    return d
def setup_inputs_edge(rng):
    d = setup_inputs(rng); d.update(lists(rng, "edge"))
    for k in ("tab",): d[k] = (d[k].astype(np.float32) * (1 / 1024.0)).astype(d[k].dtype)
    return d
def setup_inputs_full(rng):
    d = setup_inputs(rng); d.update(lists(rng, "full"))
    return d
def setup_inputs_sorted(rng):
    d = setup_inputs(rng); d.update(lists(rng, "sorted"))
    return d
def check_inputs(x):
    bad = []
    if x["idx"].min() < 0 or x["idx"].max() >= N * R: bad.append("idx out of range")
    if max(int(np.bincount(entries(a) // R, minlength=N).max()) for a in x["idx"]) > CAPP: bad.append("more than CAPP entries of a list point into one rank's part")
    return bad
def reference(tab, idx):
    A = np.concatenate(list(tab), axis=0)
    return {"y": np.stack([A[entries(idx[r])] for r in range(N)])}

@@ -1,0 +1,368 @@
+from concourse.bass import DstId, RemoteDMATransfer
+from concourse.mybir import dt, AluOpType, AxisListType, ActivationFunctionType
+
+F, I32, U16, BF = "float32", "int32", "uint16", "bfloat16"
+SCRATCH = {
+    "IDX": ("sbuf", [128, 8], I32),
+    "A": ("sbuf", [128, 4096], F),
+    "TT": ("sbuf", [128, 8192], F),
+    "G": ("sbuf", [128, 2048], F),
+    "LF": ("sbuf", [128, 4096], F),
+    "YT": ("sbuf", [128, 512], F),
+    "YS": ("sbuf", [128, 512], F),
+    "REQH": ("sbuf", [128, 512], U16),
+    "OFFALL": ("sbuf", [128, 128], U16),
+    "FOFF": ("sbuf", [128, 32], U16),
+    "IDENT": ("sbuf", [128, 128], F),
+    "LC": ("sbuf", [128, 512], F),
+    "UT": ("sbuf", [128, 128], BF),
+    "ONESB": ("sbuf", [128, 128], BF),
+    "IO16": ("sbuf", [128, 16], BF),
+    "IOM": ("sbuf", [128, 128], BF),
+    "ION": ("sbuf", [128, 128], BF),
+    "OHZ": ("sbuf", [128, 240], BF),
+    "LL": ("sbuf", [128, 1024], BF),
+    "RH": ("sbuf", [128, 1024], BF),
+    "RL": ("sbuf", [128, 1024], BF),
+    "PROD": ("sbuf", [128, 128], F),
+    "PIDX": ("sbuf", [128, 1], I32),
+    "PARI": ("sbuf", [128, 1], I32),
+    "PAR": ("sbuf", [128, 1], F),
+    "PS": ("psum", [128, 512], F),
+    "PSO": ("psum", [128, 512], F),
+    "PSF": ("psum", [128, 512], F),
+}
+for _n in ("OI", "LOI", "KA", "BQ", "CP", "SI", "K1I", "SHI", "JLI", "BI"):
+    SCRATCH[_n] = ("sbuf", [128, 8], I32)
+for _n in ("OF", "LOF", "T1", "T2", "T3", "HIF", "O8", "O128", "SF", "K1F", "K2F", "XB", "V1", "V2", "V3", "VAL"):
+    SCRATCH[_n] = ("sbuf", [128, 8], F)
+for _n in range(5):
+    SCRATCH["PT%d" % _n] = ("psum", [128, 512], F)
+
+SEMAPHORES = ["v", "a", "p", "gc", "ldi", "yst", "ls", "rqh", "rqd", "rqc", "rqr", "rqo", "rlS", "rlC",
+              "dtd", "dtc", "dtr", "dto"] + ["ld%d" % _k for _k in range(8)]
+
+
+def _bits(m):
+    return [1 << i for i in range(m.bit_length()) if (m >> i) & 1]
+
+
+def _plan(T, topo):
+    cores = list(T.cores)
+    hosts = sorted(set(topo.host(c) for c in cores))
+    RK = dict((h, [c for c in cores if topo.host(c) == h]) for h in hosts)
+    HP, nb = {}, {}
+    for h in hosts:
+        ch = topo.chip(RK[h][0])
+        free = [c for c in range(h * topo.CORES_PER_HOST, (h + 1) * topo.CORES_PER_HOST)
+                if topo.chip(c) == ch and c not in cores]
+        HP[h] = []
+        for c in RK[h]:
+            same = sorted(x for x in RK[h] if topo.die(x) == topo.die(c))
+            HP[h].append(sorted(x for x in free if topo.die(x) == topo.die(c))[same.index(c)])
+        rk = [x for x in hosts if x != h and topo.rack(x) == topo.rack(h)][0]
+        dg = [x for x in hosts if x != h and not topo.may_write(RK[h][0], RK[x][0])][0]
+        cb = [x for x in hosts if x not in (h, rk, dg)][0]
+        nb[h] = (rk, cb, dg)
+    return RK, HP, nb
+
+
+def _tr(T, topo, core, dst, mask, sem, src, out):
+    rid, pid = topo.addr(dst, core)
+    return RemoteDMATransfer(dst_ids=[DstId(rid=rid, pnc=pid)], dma_engine_mask=mask, remote_sem=T.sem[sem], src=src, dst=out)
+
+
+def _helper(g, core, T, topo, RK, HP, nb):
+    h = topo.host(core)
+    c = HP[h].index(core)
+    rk, cb, dg = nb[h]
+    E = _bits(topo.mask(core, RK[cb][0]))
+    q = T.rank_of(RK[rk][c])
+    ap = T.REQH[:, q * 32:(q + 1) * 32]
+    g.wait_ge(T.sem.rqh, len(E))
+    g.remote_dma_fused([_tr(T, topo, core, d, E[2 * i] | E[2 * i + 1], "rqd", ap, ap) for i, d in enumerate(RK[cb])],
+                       local_sem=T.sem.ls)
+    o = T.rank_of(RK[rk][c])
+    g.wait_ge(T.sem.rlS, 4)
+    g.remote_dma_fused([_tr(T, topo, core, RK[cb][i], E[4 + 2 * i] | E[5 + 2 * i], "dtd",
+                            T.G[:, i * 128:(i + 1) * 128], T.LF[:, o * 128:(o + 1) * 128]) for i in (0, 1)],
+                       local_sem=T.sem.ls)
+    o = T.rank_of(RK[cb][c])
+    g.wait_ge(T.sem.rlC, 4)
+    g.remote_dma_fused([_tr(T, topo, core, RK[rk][i], E[2 * i - 4] | E[2 * i - 3], "dtd",
+                            T.G[:, i * 128:(i + 1) * 128], T.LF[:, o * 128:(o + 1) * 128]) for i in (2, 3)],
+                       local_sem=T.sem.ls)
+    g.wait_ge(T.sem.ls, 16)
+
+
+def rank_program(g, core, T, topo):
+    RK, HP, nb = _plan(T, topo)
+    h = topo.host(core)
+    rank = T.rank_of(core)
+    if rank is None:
+        if h in HP and core in HP[h]:
+            _helper(g, core, T, topo, RK, HP, nb)
+        return
+    V, S, P, Q = g.vector, g.scalar, g.tensor, g.sync
+    QS = {"v": V, "a": S, "p": P, "q": Q, "g": g}
+    A = AluOpType
+    COPY = ActivationFunctionType.Copy
+    cnt, waited = {}, {}
+
+    def inc(ins, name, n=1):
+        ins.then_inc(T.sem[name], n)
+        cnt[name] = cnt.get(name, 0) + n
+        return cnt[name]
+
+    def wait(qn, name, n):
+        if waited.get((qn, name), 0) >= n:
+            return
+        QS[qn].wait_ge(T.sem[name], n)
+        waited[(qn, name)] = n
+
+    def vo(ins):
+        return inc(ins, "v")
+
+    def vsync():
+        wait("v", "v", cnt["v"])
+
+    c = RK[h].index(core)
+    rk, cb, dg = nb[h]
+    offE = _bits(topo.mask(core, RK[rk][0]))
+    onE = [b for b in _bits(topo.mask(core, HP[h][c])) if b not in offE]
+
+    inc(S.dma_start(T.IDX[:], T.idx[:]), "ldi", 16)
+    for k in range(8):
+        inc(Q.dma_start(T.A[:, 512 * k:512 * k + 512], T.tab[1024 * k:1024 * k + 1024, :]), "ld%d" % k, 16)
+
+    m_id = vo(V.memset(T.IDENT[:], 1.0))
+    m_ut = vo(V.memset(T.UT[:], 1.0))
+    vo(V.memset(T.ONESB[:], 1.0))
+    m_z = vo(V.memset(T.OHZ[:, 0:112], 0.0))
+    m_lc = vo(V.memset(T.LC[:], 1.0))
+    wait("g", "v", m_id)
+    g_id = inc(g.affine_select(T.IDENT[:], T.IDENT[:], [[-1, 128]], A.is_equal, 0.0, 0, 1), "gc")
+    g_16 = inc(g.iota(T.IO16[:], [[1, 16]], 0, 0, allow_small_or_imprecise_dtypes=True), "gc")
+    wait("g", "v", m_ut)
+    g_ut = inc(g.affine_select(T.UT[:], T.UT[:], [[1, 128]], A.is_ge, 0.0, -1, -1), "gc")
+    inc(g.iota(T.IOM[:], [[16, 2], [0, 4], [1, 16]], 0, 0, allow_small_or_imprecise_dtypes=True), "gc")
+    g_n = inc(g.iota(T.ION[:], [[1, 128]], 0, 0, allow_small_or_imprecise_dtypes=True), "gc")
+    g_p = inc(g.iota(T.PIDX[:], [[0, 1]], 0, 1), "gc")
+    wait("g", "v", m_lc)
+    g_lc = inc(g.affine_select(T.LC[:], T.LC[:], [[-1, 8], [0, 4], [-8, 16]], A.is_equal, 0.0, 0, 1), "gc")
+
+    wait("v", "ldi", 16)
+    vo(V.tensor_scalar(T.OI[:], T.IDX[:], 13, None, A.logical_shift_right))
+    vsync()
+    vo(V.tensor_copy(T.OF[:], T.OI[:]))
+    vsync()
+    wait("v", "gc", g_16)
+    for j in range(8):
+        n_oh = vo(V.tensor_scalar(T.OHZ[:, 112 + 16 * j:128 + 16 * j], T.IO16[:], T.OF[:, j:j + 1], None, A.is_equal))
+    vo(V.tensor_scalar(T.LOI[:], T.IDX[:], 3, 127, A.logical_shift_right, A.bitwise_and))
+    vo(V.tensor_scalar(T.KA[:], T.IDX[:], 1, 0xE00, A.logical_shift_right, A.bitwise_and))
+    vo(V.tensor_scalar(T.BQ[:], T.IDX[:], 7, None, A.bitwise_and))
+    vo(V.tensor_scalar(T.CP[:], T.IDX[:], 1, None, A.bitwise_and))
+    vo(V.tensor_scalar(T.O8[:], T.OF[:], 8.0, None, A.mult))
+    vo(V.tensor_scalar(T.O128[:], T.OF[:], 128.0, None, A.mult))
+    vsync()
+    vo(V.tensor_copy(T.LOF[:], T.LOI[:]))
+    vo(V.tensor_scalar(T.T1[:], T.BQ[:], 64.0, None, A.mult))
+    vo(V.tensor_scalar(T.T2[:], T.CP[:], 4032.0, None, A.mult))
+    vsync()
+    vo(V.tensor_tensor(T.T3[:], T.T1[:], T.T2[:], A.add))
+    vsync()
+    vo(V.tensor_tensor(T.HIF[:], T.T3[:], T.KA[:], A.add))
+    wait("v", "gc", g_p)
+    vo(V.tensor_scalar(T.PARI[:], T.PIDX[:], 1, None, A.bitwise_and))
+    vsync()
+    vo(V.tensor_copy(T.PAR[:], T.PARI[:]))
+
+    pun, evd, st = {}, {}, {}
+
+    def prefix():
+        wait("p", "v", n_oh)
+        wait("p", "gc", g_ut)
+        P.matmul(T.PS[:, 0:128], T.UT[:], T.OHZ[:, 112:240], True, False)
+        for d in range(1, 8):
+            ins = P.matmul(T.PS[:, 0:128], T.ONESB[:], T.OHZ[:, 112 - 16 * d:240 - 16 * d], False, d == 7)
+        pp = inc(ins, "p")
+        wait("v", "p", pp)
+        vsync()
+        vo(V.tensor_tensor(T.PROD[:], T.OHZ[:, 112:240], T.PS[:, 0:128], A.mult))
+        vsync()
+        for j in range(8):
+            vo(V.tensor_reduce(T.SF[:, j:j + 1], T.PROD[:, 16 * j:16 * j + 16], AxisListType.X, A.add))
+        vsync()
+        vo(V.tensor_copy(T.SI[:], T.SF[:]))
+        vsync()
+        vo(V.tensor_scalar(T.K1I[:], T.SI[:], 31, None, A.bitwise_and))
+        vo(V.tensor_scalar(T.SHI[:], T.SI[:], 5, None, A.logical_shift_right))
+        vsync()
+        vo(V.tensor_copy(T.K1F[:], T.K1I[:]))
+        vo(V.tensor_tensor(T.K2F[:], T.O8[:], T.SHI[:], A.add))
+        vsync()
+        wait("v", "gc", g_n)
+        st["nj"] = []
+        for j in range(8):
+            sl = slice(128 * j, 128 * j + 128)
+            vo(V.tensor_scalar(T.LL[:, sl], T.IOM[:], T.K1F[:, j:j + 1], None, A.is_equal))
+            vo(V.tensor_scalar(T.RH[:, sl], T.ION[:], T.K2F[:, j:j + 1], T.HIF[:, j:j + 1], A.is_equal, A.mult))
+            st["nj"].append(vo(V.tensor_scalar(T.RL[:, sl], T.ION[:], T.K2F[:, j:j + 1], T.LOF[:, j:j + 1], A.is_equal, A.mult)))
+
+    def offsets():
+        for j in range(8):
+            sl = slice(128 * j, 128 * j + 128)
+            wait("p", "v", st["nj"][j])
+            P.matmul(T.PSO[:, 0:128], T.LL[:, sl], T.RH[:, sl], j == 0, False)
+            ins = P.matmul(T.PSO[:, 0:128], T.LL[:, sl], T.RL[:, sl], False, j == 7)
+        po = inc(ins, "p")
+        wait("v", "p", po)
+        st["noff"] = vo(V.tensor_copy(T.OFFALL[:], T.PSO[:, 0:128]))
+        wait("g", "v", st["noff"])
+        hp = HP[rk][c]
+        rid, pid = topo.addr(hp, core)
+        m = 0
+        for b in offE:
+            m |= b
+        r0 = T.rank_of(RK[dg][0])
+        g.remote_dma(T.REQH[:, rank * 32:rank * 32 + 32], T.OFFALL[:, r0 * 8:r0 * 8 + 32], T.sem.rqh, T.sem.ls, pid, rid, m)
+        cnt["ls"] = cnt.get("ls", 0) + len(offE)
+        trs = []
+        for hx, sem, e0 in ((rk, "rqr", 0), (cb, "rqc", 4)):
+            r0 = T.rank_of(RK[hx][0])
+            for i, d in enumerate(RK[hx]):
+                trs.append(_tr(T, topo, core, d, offE[e0 + i], sem, T.OFFALL[:, r0 * 8:r0 * 8 + 32],
+                               T.REQH[:, rank * 32:rank * 32 + 32]))
+                cnt["ls"] += 1
+        r0 = T.rank_of(RK[h][0])
+        for i, d in enumerate(x for x in RK[h] if x != core):
+            trs.append(_tr(T, topo, core, d, onE[2 * i] | onE[2 * i + 1], "rqo", T.OFFALL[:, r0 * 8:r0 * 8 + 32],
+                           T.REQH[:, rank * 32:rank * 32 + 32]))
+            cnt["ls"] += 2
+        g.remote_dma_fused(trs, local_sem=T.sem.ls)
+        vo(V.tensor_scalar(T.JLI[:], T.SI[:], 15, None, A.bitwise_and))
+        vo(V.tensor_scalar(T.BI[:], T.SI[:], 4, 1, A.logical_shift_right, A.bitwise_and))
+        vo(V.tensor_scalar(T.V1[:], T.SHI[:], 16.0, None, A.mult))
+        vsync()
+        vo(V.tensor_scalar(T.XB[:], T.BI[:], T.PAR[:, 0:1], 2048.0, A.not_equal, A.mult))
+        vo(V.tensor_tensor(T.V2[:], T.V1[:], T.JLI[:], A.add))
+        vsync()
+        vo(V.tensor_tensor(T.V3[:], T.V2[:], T.O128[:], A.add))
+        vsync()
+        st["nval"] = vo(V.tensor_tensor(T.VAL[:], T.V3[:], T.XB[:], A.add))
+
+    def cp(e, out, in_):
+        if e == "v":
+            return inc(V.tensor_copy(out, in_), "v")
+        return inc(S.activation(out, in_, COPY), "a")
+
+    wait("p", "gc", g_id)
+    for w in range(16):
+        if w % 2 == 0:
+            wait("p", "ld%d" % (w // 2), 16)
+        if w >= 5:
+            wait("p", evd[w - 5][0], evd[w - 5][1])
+        pt = T["PT%d" % (w % 5)]
+        for x in (0, 1):
+            u = 2 * w + x
+            ins = P.transpose(pt[:, 128 * x:128 * x + 128], T.A[:, 128 * u:128 * u + 128], T.IDENT[:])
+        pun[w] = inc(ins, "p")
+        e = "v" if (w >= 9 and w % 2 == 1) else "a"
+        wait(e, "p", pun[w])
+        lo, hi = slice(256 * w, 256 * w + 256), slice(4096 + 256 * w, 4096 + 256 * w + 256)
+        cp(e, T.TT[0:64, lo], pt[0:64, 0:256])
+        cp(e, T.TT[64:128, lo], pt[0:64, 0:256])
+        cp(e, T.TT[64:128, hi], pt[64:128, 0:256])
+        evd[w] = (e, cp(e, T.TT[0:64, hi], pt[64:128, 0:256]))
+        if w == 1:
+            prefix()
+        if w == 5:
+            offsets()
+    ttv, tta = cnt["v"], cnt["a"]
+    wait("p", "v", st["nval"])
+    wait("p", "gc", g_lc)
+    for k in range(4):
+        ins = P.matmul(T.PSF[:, 8 * k:8 * k + 8], T.LC[:, 128 * k:128 * k + 128], T.VAL[:], True, True)
+    pf = inc(ins, "p")
+
+    for e in ("v", "a"):
+        wait(e, "v", ttv)
+        wait(e, "a", tta)
+    done = {}
+    for hx, sem, tot in ((dg, "rqd", 8), (cb, "rqc", 4), (rk, "rqr", 4), (h, "rqo", 6)):
+        for i, qc in enumerate(RK[hx]):
+            e = "v" if i < 2 else "a"
+            wait(e, sem, tot)
+            q = T.rank_of(qc)
+            if qc == core:
+                cp(e, T.LF[:, q * 128:q * 128 + 128], T.TT[:, 0:8192].indirect(T.OFFALL[:, 8 * q:8 * q + 8]))
+            else:
+                cp(e, T.G[:, q * 128:q * 128 + 128], T.TT[:, 0:8192].indirect(T.REQH[:, 32 * q + 8 * c:32 * q + 8 * c + 8]))
+        done[hx] = (cnt["v"], cnt["a"])
+
+    def gwait(hx):
+        wait("g", "v", done[hx][0])
+        wait("g", "a", done[hx][1])
+
+    def piece(qc):
+        q = T.rank_of(qc)
+        return T.G[:, q * 128:q * 128 + 128]
+
+    mine = T.LF[:, rank * 128:rank * 128 + 128]
+    gwait(dg)
+    trs = []
+    for i, qc in enumerate(RK[dg]):
+        hp, sem = (HP[rk][c], "rlS") if i < 2 else (HP[cb][c], "rlC")
+        trs.append(_tr(T, topo, core, hp, offE[2 * i] | offE[2 * i + 1], sem, piece(qc), T.G[:, i * 128:i * 128 + 128]))
+        cnt["ls"] += 2
+    g.remote_dma_fused(trs, local_sem=T.sem.ls)
+    gwait(cb)
+    gwait(rk)
+    trs = []
+    for hx, sem, e0 in ((rk, "dtr", 0), (cb, "dtc", 4)):
+        for i, qc in enumerate(RK[hx]):
+            trs.append(_tr(T, topo, core, qc, offE[e0 + i], sem, piece(qc), mine))
+            cnt["ls"] += 1
+    g.remote_dma_fused(trs, local_sem=T.sem.ls)
+    gwait(h)
+    trs = []
+    for i, qc in enumerate(x for x in RK[h] if x != core):
+        trs.append(_tr(T, topo, core, qc, onE[2 * i] | onE[2 * i + 1], "dto", piece(qc), mine))
+        cnt["ls"] += 2
+    g.remote_dma_fused(trs, local_sem=T.sem.ls)
+
+    wait("v", "p", pf)
+    n_fo = vo(V.tensor_copy(T.FOFF[:], T.PSF[:, 0:32]))
+    for hx, sem, tot in ((h, "dto", 6), (rk, "dtr", 4), (cb, "dtc", 4), (dg, "dtd", 8)):
+        c0 = T.rank_of(RK[hx][0]) * 128
+        for e in ("v", "a"):
+            wait(e, sem, tot)
+            if hx == h:
+                wait(e, "v", done[h][0])
+                wait(e, "a", done[h][1])
+        cp("v", T.LF[64:128, 2048 + c0:2048 + c0 + 512], T.LF[0:64, c0:c0 + 512])
+        cp("a", T.LF[0:64, 2048 + c0:2048 + c0 + 512], T.LF[64:128, c0:c0 + 512])
+    cv, ca = cnt["v"], cnt["a"]
+    gd = {}
+    for e in ("v", "a"):
+        wait(e, "v", cv)
+        wait(e, "a", ca)
+    for k in range(4):
+        e = "v" if k % 2 == 0 else "a"
+        gd[k] = (e, cp(e, T.YT[:, 128 * k:128 * k + 128], T.LF[:, 0:4096].indirect(T.FOFF[:, 8 * k:8 * k + 8])))
+    wait("p", "v", cv)
+    wait("p", "a", ca)
+    for k in range(4):
+        e = gd[k][0]
+        wait("p", e, gd[k][1])
+        pk = inc(P.transpose(T["PT%d" % k][:, 0:128], T.YT[:, 128 * k:128 * k + 128], T.IDENT[:]), "p")
+        wait(e, "p", pk)
+        cp(e, T.YS[:, 128 * k:128 * k + 128], T["PT%d" % k][:, 0:128])
+    wait("q", "v", cnt["v"])
+    wait("q", "a", cnt["a"])
+    inc(Q.dma_start(T.y[:, :], T.YS[:]), "yst", 16)
+    for name in sorted(cnt):
+        if name != "yst":
+            wait("g", name, cnt[name])
+    wait("g", "yst", 16)

@@ -40,11 +40,24 @@ for _n in range(5):
     SCRATCH["PT%d" % _n] = ("psum", [128, 512], F)
 
 SEMAPHORES = ["v", "a", "p", "gc", "ldi", "yst", "ls", "rqh", "rqd", "rqc", "rqr", "rqo", "rlS", "rlC",
-              "dtd", "dtc", "dtr", "dto"] + ["ld%d" % _k for _k in range(8)]
+              "dtd", "dtc", "dtr", "dto", "tb", "go"] + ["ld%d" % _k for _k in range(8)] + ["ta%d" % _k for _k in range(8)]
+
+NW = 12
+
+
+def _handed():
+    return [(k, max(512 * k, 256 * NW), 512 * k + 512) for k in sorted(set(w // 2 for w in range(NW, 16)))]
 
 
 def _bits(m):
     return [1 << i for i in range(m.bit_length()) if (m >> i) & 1]
+
+
+def _or(bits):
+    m = 0
+    for b in bits:
+        m |= b
+    return m
 
 
 def _plan(T, topo):
@@ -76,6 +89,43 @@ def _helper(g, core, T, topo, RK, HP, nb):
     h = topo.host(core)
     c = HP[h].index(core)
     rk, cb, dg = nb[h]
+    V, S, P = g.vector, g.scalar, g.tensor
+    me = RK[h][c]
+    B = _bits(topo.mask(core, me))
+    hb = len(B) // 2
+    V.memset(T.IDENT[:], 1.0).then_inc(T.sem["v"], 1)
+    g.wait_ge(T.sem["v"], 1)
+    g.affine_select(T.IDENT[:], T.IDENT[:], [[-1, 128]], AluOpType.is_equal, 0.0, 0, 1).then_inc(T.sem["gc"], 1)
+    P.wait_ge(T.sem["gc"], 1)
+    n = {"v": 1, "a": 0, "p": 0}
+    marks = {}
+    for w in range(NW, 16):
+        if w == NW or w % 2 == 0:
+            P.wait_ge(T.sem["ta%d" % (w // 2)], hb)
+        pt = T["PT%d" % (w - NW)]
+        for x in (0, 1):
+            u = 2 * w + x
+            ins = P.transpose(pt[:, 128 * x:128 * x + 128], T.A[:, 128 * u:128 * u + 128], T.IDENT[:])
+        ins.then_inc(T.sem["p"], 1)
+        n["p"] += 1
+        e = "v" if (w - NW) % 2 == 0 else "a"
+        (V if e == "v" else S).wait_ge(T.sem["p"], n["p"])
+        lo, hi = slice(256 * w, 256 * w + 256), slice(4096 + 256 * w, 4096 + 256 * w + 256)
+        for out, in_ in ((T.TT[0:64, lo], pt[0:64, 0:256]), (T.TT[64:128, lo], pt[0:64, 0:256]),
+                         (T.TT[64:128, hi], pt[64:128, 0:256]), (T.TT[0:64, hi], pt[64:128, 0:256])):
+            if e == "v":
+                V.tensor_copy(out, in_).then_inc(T.sem["v"], 1)
+            else:
+                S.activation(out, in_, ActivationFunctionType.Copy).then_inc(T.sem["a"], 1)
+            n[e] += 1
+        marks[w] = (n["v"], n["a"])
+    for k, a0, b0 in _handed():
+        g.wait_ge(T.sem["v"], marks[2 * k + 1][0])
+        if marks[2 * k + 1][1]:
+            g.wait_ge(T.sem["a"], marks[2 * k + 1][1])
+        g.remote_dma_fused([_tr(T, topo, core, me, _or(B[hb:]), "tb", T.TT[:, a0:b0], T.TT[:, a0:b0]),
+                            _tr(T, topo, core, me, _or(B[:hb]), "tb", T.TT[:, 4096 + a0:4096 + b0],
+                                T.TT[:, 4096 + a0:4096 + b0])], local_sem=T.sem.ls)
     E = _bits(topo.mask(core, RK[cb][0]))
     q = T.rank_of(RK[rk][c])
     ap = T.REQH[:, q * 32:(q + 1) * 32]
@@ -92,7 +142,7 @@ def _helper(g, core, T, topo, RK, HP, nb):
     g.remote_dma_fused([_tr(T, topo, core, RK[rk][i], E[2 * i - 4] | E[2 * i - 3], "dtd",
                             T.G[:, i * 128:(i + 1) * 128], T.LF[:, o * 128:(o + 1) * 128]) for i in (2, 3)],
                        local_sem=T.sem.ls)
-    g.wait_ge(T.sem.ls, 16)
+    g.wait_ge(T.sem.ls, 16 + len(B) * len(_handed()))
 
 
 def rank_program(g, core, T, topo):
@@ -132,7 +182,16 @@ def rank_program(g, core, T, topo):
     onE = [b for b in _bits(topo.mask(core, HP[h][c])) if b not in offE]
 
     inc(S.dma_start(T.IDX[:], T.idx[:]), "ldi", 16)
-    for k in range(8):
+    hc = [k for k, a0, b0 in _handed()]
+    rc = [k for k in range(8) if 2 * k < NW and k not in hc]
+    first = []
+    for i in range(max(len(hc), 3)):
+        first += rc[i:i + 1] if i < 3 else []
+        first += hc[i:i + 1]
+    for k in first + [None] + [k for k in rc if k not in first]:
+        if k is None:
+            Q.wait_ge(T.sem.go, 1)
+            continue
         inc(Q.dma_start(T.A[:, 512 * k:512 * k + 512], T.tab[1024 * k:1024 * k + 1024, :]), "ld%d" % k, 16)
 
     m_id = vo(V.memset(T.IDENT[:], 1.0))
@@ -148,6 +207,13 @@ def rank_program(g, core, T, topo):
     inc(g.iota(T.IOM[:], [[16, 2], [0, 4], [1, 16]], 0, 0, allow_small_or_imprecise_dtypes=True), "gc")
     g_n = inc(g.iota(T.ION[:], [[1, 128]], 0, 0, allow_small_or_imprecise_dtypes=True), "gc")
     g_p = inc(g.iota(T.PIDX[:], [[0, 1]], 0, 1), "gc")
+    rid, pid = topo.addr(HP[h][c], core)
+    for i, (k, a0, b0) in enumerate(_handed()):
+        wait("g", "ld%d" % k, 16)
+        eng = onE if i % 2 == 0 else offE
+        g.remote_dma(T.A[:, a0:b0], T.A[:, a0:b0], T.sem["ta%d" % k], T.sem.ls, pid, rid, _or(eng))
+        cnt["ls"] = cnt.get("ls", 0) + len(eng)
+    g.sem_inc(T.sem.go, 1)
     wait("g", "v", m_lc)
     g_lc = inc(g.affine_select(T.LC[:], T.LC[:], [[-1, 8], [0, 4], [-8, 16]], A.is_equal, 0.0, 0, 1), "gc")
 
@@ -222,11 +288,9 @@ def rank_program(g, core, T, topo):
         wait("g", "v", st["noff"])
         hp = HP[rk][c]
         rid, pid = topo.addr(hp, core)
-        m = 0
-        for b in offE:
-            m |= b
         r0 = T.rank_of(RK[dg][0])
-        g.remote_dma(T.REQH[:, rank * 32:rank * 32 + 32], T.OFFALL[:, r0 * 8:r0 * 8 + 32], T.sem.rqh, T.sem.ls, pid, rid, m)
+        g.remote_dma(T.REQH[:, rank * 32:rank * 32 + 32], T.OFFALL[:, r0 * 8:r0 * 8 + 32], T.sem.rqh, T.sem.ls, pid, rid,
+                     _or(offE))
         cnt["ls"] = cnt.get("ls", 0) + len(offE)
         trs = []
         for hx, sem, e0 in ((rk, "rqr", 0), (cb, "rqc", 4)):
@@ -258,7 +322,7 @@ def rank_program(g, core, T, topo):
         return inc(S.activation(out, in_, COPY), "a")
 
     wait("p", "gc", g_id)
-    for w in range(16):
+    for w in range(NW):
         if w % 2 == 0:
             wait("p", "ld%d" % (w // 2), 16)
         if w >= 5:
@@ -289,6 +353,7 @@ def rank_program(g, core, T, topo):
     for e in ("v", "a"):
         wait(e, "v", ttv)
         wait(e, "a", tta)
+        wait(e, "tb", (len(onE) + len(offE)) * len(_handed()))
     done = {}
     for hx, sem, tot in ((dg, "rqd", 8), (cb, "rqc", 4), (rk, "rqr", 4), (h, "rqo", 6)):
         for i, qc in enumerate(RK[hx]):

from concourse.bass import DstId, RemoteDMATransfer
from concourse.mybir import dt, AluOpType, AxisListType, ActivationFunctionType

F, I32, U16, BF = "float32", "int32", "uint16", "bfloat16"
SCRATCH = {
    "IDX": ("sbuf", [128, 8], I32),
    "A": ("sbuf", [128, 4096], F),
    "TT": ("sbuf", [128, 8192], F),
    "G": ("sbuf", [128, 2048], F),
    "LF": ("sbuf", [128, 4096], F),
    "YT": ("sbuf", [128, 512], F),
    "YS": ("sbuf", [128, 512], F),
    "REQH": ("sbuf", [128, 512], U16),
    "OFFALL": ("sbuf", [128, 128], U16),
    "FOFF": ("sbuf", [128, 32], U16),
    "IDENT": ("sbuf", [128, 128], F),
    "LC": ("sbuf", [128, 512], F),
    "UT": ("sbuf", [128, 128], BF),
    "ONESB": ("sbuf", [128, 128], BF),
    "IO16": ("sbuf", [128, 16], BF),
    "IOM": ("sbuf", [128, 128], BF),
    "ION": ("sbuf", [128, 128], BF),
    "OHZ": ("sbuf", [128, 240], BF),
    "LL": ("sbuf", [128, 1024], BF),
    "RH": ("sbuf", [128, 1024], BF),
    "RL": ("sbuf", [128, 1024], BF),
    "PROD": ("sbuf", [128, 128], F),
    "PIDX": ("sbuf", [128, 1], I32),
    "PARI": ("sbuf", [128, 1], I32),
    "PAR": ("sbuf", [128, 1], F),
    "PS": ("psum", [128, 512], F),
    "PSO": ("psum", [128, 512], F),
    "PSF": ("psum", [128, 512], F),
}
for _n in ("OI", "LOI", "KA", "BQ", "CP", "SI", "K1I", "SHI", "JLI", "BI"):
    SCRATCH[_n] = ("sbuf", [128, 8], I32)
for _n in ("OF", "LOF", "T1", "T2", "T3", "HIF", "O8", "O128", "SF", "K1F", "K2F", "XB", "V1", "V2", "V3", "VAL"):
    SCRATCH[_n] = ("sbuf", [128, 8], F)
for _n in range(5):
    SCRATCH["PT%d" % _n] = ("psum", [128, 512], F)

SEMAPHORES = ["v", "a", "p", "gc", "ldi", "yst", "ls", "rqh", "rqd", "rqc", "rqr", "rqo", "rlS", "rlC",
              "dtd", "dtc", "dtr", "dto", "tb", "go"] + ["ld%d" % _k for _k in range(8)] + ["ta%d" % _k for _k in range(8)]

NW = 12


def _handed():
    return [(k, max(512 * k, 256 * NW), 512 * k + 512) for k in sorted(set(w // 2 for w in range(NW, 16)))]


def _bits(m):
    return [1 << i for i in range(m.bit_length()) if (m >> i) & 1]


def _or(bits):
    m = 0
    for b in bits:
        m |= b
    return m


def _plan(T, topo):
    cores = list(T.cores)
    hosts = sorted(set(topo.host(c) for c in cores))
    RK = dict((h, [c for c in cores if topo.host(c) == h]) for h in hosts)
    HP, nb = {}, {}
    for h in hosts:
        ch = topo.chip(RK[h][0])
        free = [c for c in range(h * topo.CORES_PER_HOST, (h + 1) * topo.CORES_PER_HOST)
                if topo.chip(c) == ch and c not in cores]
        HP[h] = []
        for c in RK[h]:
            same = sorted(x for x in RK[h] if topo.die(x) == topo.die(c))
            HP[h].append(sorted(x for x in free if topo.die(x) == topo.die(c))[same.index(c)])
        rk = [x for x in hosts if x != h and topo.rack(x) == topo.rack(h)][0]
        dg = [x for x in hosts if x != h and not topo.may_write(RK[h][0], RK[x][0])][0]
        cb = [x for x in hosts if x not in (h, rk, dg)][0]
        nb[h] = (rk, cb, dg)
    return RK, HP, nb


def _tr(T, topo, core, dst, mask, sem, src, out):
    rid, pid = topo.addr(dst, core)
    return RemoteDMATransfer(dst_ids=[DstId(rid=rid, pnc=pid)], dma_engine_mask=mask, remote_sem=T.sem[sem], src=src, dst=out)


def _helper(g, core, T, topo, RK, HP, nb):
    h = topo.host(core)
    c = HP[h].index(core)
    rk, cb, dg = nb[h]
    V, S, P = g.vector, g.scalar, g.tensor
    me = RK[h][c]
    B = _bits(topo.mask(core, me))
    hb = len(B) // 2
    V.memset(T.IDENT[:], 1.0).then_inc(T.sem["v"], 1)
    g.wait_ge(T.sem["v"], 1)
    g.affine_select(T.IDENT[:], T.IDENT[:], [[-1, 128]], AluOpType.is_equal, 0.0, 0, 1).then_inc(T.sem["gc"], 1)
    P.wait_ge(T.sem["gc"], 1)
    n = {"v": 1, "a": 0, "p": 0}
    marks = {}
    for w in range(NW, 16):
        if w == NW or w % 2 == 0:
            P.wait_ge(T.sem["ta%d" % (w // 2)], hb)
        pt = T["PT%d" % (w - NW)]
        for x in (0, 1):
            u = 2 * w + x
            ins = P.transpose(pt[:, 128 * x:128 * x + 128], T.A[:, 128 * u:128 * u + 128], T.IDENT[:])
        ins.then_inc(T.sem["p"], 1)
        n["p"] += 1
        e = "v" if (w - NW) % 2 == 0 else "a"
        (V if e == "v" else S).wait_ge(T.sem["p"], n["p"])
        lo, hi = slice(256 * w, 256 * w + 256), slice(4096 + 256 * w, 4096 + 256 * w + 256)
        for out, in_ in ((T.TT[0:64, lo], pt[0:64, 0:256]), (T.TT[64:128, lo], pt[0:64, 0:256]),
                         (T.TT[64:128, hi], pt[64:128, 0:256]), (T.TT[0:64, hi], pt[64:128, 0:256])):
            if e == "v":
                V.tensor_copy(out, in_).then_inc(T.sem["v"], 1)
            else:
                S.activation(out, in_, ActivationFunctionType.Copy).then_inc(T.sem["a"], 1)
            n[e] += 1
        marks[w] = (n["v"], n["a"])
    for k, a0, b0 in _handed():
        g.wait_ge(T.sem["v"], marks[2 * k + 1][0])
        if marks[2 * k + 1][1]:
            g.wait_ge(T.sem["a"], marks[2 * k + 1][1])
        g.remote_dma_fused([_tr(T, topo, core, me, _or(B[hb:]), "tb", T.TT[:, a0:b0], T.TT[:, a0:b0]),
                            _tr(T, topo, core, me, _or(B[:hb]), "tb", T.TT[:, 4096 + a0:4096 + b0],
                                T.TT[:, 4096 + a0:4096 + b0])], local_sem=T.sem.ls)
    E = _bits(topo.mask(core, RK[cb][0]))
    q = T.rank_of(RK[rk][c])
    ap = T.REQH[:, q * 32:(q + 1) * 32]
    g.wait_ge(T.sem.rqh, len(E))
    g.remote_dma_fused([_tr(T, topo, core, d, E[2 * i] | E[2 * i + 1], "rqd", ap, ap) for i, d in enumerate(RK[cb])],
                       local_sem=T.sem.ls)
    o = T.rank_of(RK[rk][c])
    g.wait_ge(T.sem.rlS, 4)
    g.remote_dma_fused([_tr(T, topo, core, RK[cb][i], E[4 + 2 * i] | E[5 + 2 * i], "dtd",
                            T.G[:, i * 128:(i + 1) * 128], T.LF[:, o * 128:(o + 1) * 128]) for i in (0, 1)],
                       local_sem=T.sem.ls)
    o = T.rank_of(RK[cb][c])
    g.wait_ge(T.sem.rlC, 4)
    g.remote_dma_fused([_tr(T, topo, core, RK[rk][i], E[2 * i - 4] | E[2 * i - 3], "dtd",
                            T.G[:, i * 128:(i + 1) * 128], T.LF[:, o * 128:(o + 1) * 128]) for i in (2, 3)],
                       local_sem=T.sem.ls)
    g.wait_ge(T.sem.ls, 16 + len(B) * len(_handed()))


def rank_program(g, core, T, topo):
    RK, HP, nb = _plan(T, topo)
    h = topo.host(core)
    rank = T.rank_of(core)
    if rank is None:
        if h in HP and core in HP[h]:
            _helper(g, core, T, topo, RK, HP, nb)
        return
    V, S, P, Q = g.vector, g.scalar, g.tensor, g.sync
    QS = {"v": V, "a": S, "p": P, "q": Q, "g": g}
    A = AluOpType
    COPY = ActivationFunctionType.Copy
    cnt, waited = {}, {}

    def inc(ins, name, n=1):
        ins.then_inc(T.sem[name], n)
        cnt[name] = cnt.get(name, 0) + n
        return cnt[name]

    def wait(qn, name, n):
        if waited.get((qn, name), 0) >= n:
            return
        QS[qn].wait_ge(T.sem[name], n)
        waited[(qn, name)] = n

    def vo(ins):
        return inc(ins, "v")

    def vsync():
        wait("v", "v", cnt["v"])

    c = RK[h].index(core)
    rk, cb, dg = nb[h]
    offE = _bits(topo.mask(core, RK[rk][0]))
    onE = [b for b in _bits(topo.mask(core, HP[h][c])) if b not in offE]

    inc(S.dma_start(T.IDX[:], T.idx[:]), "ldi", 16)
    hc = [k for k, a0, b0 in _handed()]
    rc = [k for k in range(8) if 2 * k < NW and k not in hc]
    first = []
    for i in range(max(len(hc), 3)):
        first += rc[i:i + 1] if i < 3 else []
        first += hc[i:i + 1]
    for k in first + [None] + [k for k in rc if k not in first]:
        if k is None:
            Q.wait_ge(T.sem.go, 1)
            continue
        inc(Q.dma_start(T.A[:, 512 * k:512 * k + 512], T.tab[1024 * k:1024 * k + 1024, :]), "ld%d" % k, 16)

    m_id = vo(V.memset(T.IDENT[:], 1.0))
    m_ut = vo(V.memset(T.UT[:], 1.0))
    vo(V.memset(T.ONESB[:], 1.0))
    m_z = vo(V.memset(T.OHZ[:, 0:112], 0.0))
    m_lc = vo(V.memset(T.LC[:], 1.0))
    wait("g", "v", m_id)
    g_id = inc(g.affine_select(T.IDENT[:], T.IDENT[:], [[-1, 128]], A.is_equal, 0.0, 0, 1), "gc")
    g_16 = inc(g.iota(T.IO16[:], [[1, 16]], 0, 0, allow_small_or_imprecise_dtypes=True), "gc")
    wait("g", "v", m_ut)
    g_ut = inc(g.affine_select(T.UT[:], T.UT[:], [[1, 128]], A.is_ge, 0.0, -1, -1), "gc")
    inc(g.iota(T.IOM[:], [[16, 2], [0, 4], [1, 16]], 0, 0, allow_small_or_imprecise_dtypes=True), "gc")
    g_n = inc(g.iota(T.ION[:], [[1, 128]], 0, 0, allow_small_or_imprecise_dtypes=True), "gc")
    g_p = inc(g.iota(T.PIDX[:], [[0, 1]], 0, 1), "gc")
    rid, pid = topo.addr(HP[h][c], core)
    for i, (k, a0, b0) in enumerate(_handed()):
        wait("g", "ld%d" % k, 16)
        eng = onE if i % 2 == 0 else offE
        g.remote_dma(T.A[:, a0:b0], T.A[:, a0:b0], T.sem["ta%d" % k], T.sem.ls, pid, rid, _or(eng))
        cnt["ls"] = cnt.get("ls", 0) + len(eng)
    g.sem_inc(T.sem.go, 1)
    wait("g", "v", m_lc)
    g_lc = inc(g.affine_select(T.LC[:], T.LC[:], [[-1, 8], [0, 4], [-8, 16]], A.is_equal, 0.0, 0, 1), "gc")

    wait("v", "ldi", 16)
    vo(V.tensor_scalar(T.OI[:], T.IDX[:], 13, None, A.logical_shift_right))
    vsync()
    vo(V.tensor_copy(T.OF[:], T.OI[:]))
    vsync()
    wait("v", "gc", g_16)
    for j in range(8):
        n_oh = vo(V.tensor_scalar(T.OHZ[:, 112 + 16 * j:128 + 16 * j], T.IO16[:], T.OF[:, j:j + 1], None, A.is_equal))
    vo(V.tensor_scalar(T.LOI[:], T.IDX[:], 3, 127, A.logical_shift_right, A.bitwise_and))
    vo(V.tensor_scalar(T.KA[:], T.IDX[:], 1, 0xE00, A.logical_shift_right, A.bitwise_and))
    vo(V.tensor_scalar(T.BQ[:], T.IDX[:], 7, None, A.bitwise_and))
    vo(V.tensor_scalar(T.CP[:], T.IDX[:], 1, None, A.bitwise_and))
    vo(V.tensor_scalar(T.O8[:], T.OF[:], 8.0, None, A.mult))
    vo(V.tensor_scalar(T.O128[:], T.OF[:], 128.0, None, A.mult))
    vsync()
    vo(V.tensor_copy(T.LOF[:], T.LOI[:]))
    vo(V.tensor_scalar(T.T1[:], T.BQ[:], 64.0, None, A.mult))
    vo(V.tensor_scalar(T.T2[:], T.CP[:], 4032.0, None, A.mult))
    vsync()
    vo(V.tensor_tensor(T.T3[:], T.T1[:], T.T2[:], A.add))
    vsync()
    vo(V.tensor_tensor(T.HIF[:], T.T3[:], T.KA[:], A.add))
    wait("v", "gc", g_p)
    vo(V.tensor_scalar(T.PARI[:], T.PIDX[:], 1, None, A.bitwise_and))
    vsync()
    vo(V.tensor_copy(T.PAR[:], T.PARI[:]))

    pun, evd, st = {}, {}, {}

    def prefix():
        wait("p", "v", n_oh)
        wait("p", "gc", g_ut)
        P.matmul(T.PS[:, 0:128], T.UT[:], T.OHZ[:, 112:240], True, False)
        for d in range(1, 8):
            ins = P.matmul(T.PS[:, 0:128], T.ONESB[:], T.OHZ[:, 112 - 16 * d:240 - 16 * d], False, d == 7)
        pp = inc(ins, "p")
        wait("v", "p", pp)
        vsync()
        vo(V.tensor_tensor(T.PROD[:], T.OHZ[:, 112:240], T.PS[:, 0:128], A.mult))
        vsync()
        for j in range(8):
            vo(V.tensor_reduce(T.SF[:, j:j + 1], T.PROD[:, 16 * j:16 * j + 16], AxisListType.X, A.add))
        vsync()
        vo(V.tensor_copy(T.SI[:], T.SF[:]))
        vsync()
        vo(V.tensor_scalar(T.K1I[:], T.SI[:], 31, None, A.bitwise_and))
        vo(V.tensor_scalar(T.SHI[:], T.SI[:], 5, None, A.logical_shift_right))
        vsync()
        vo(V.tensor_copy(T.K1F[:], T.K1I[:]))
        vo(V.tensor_tensor(T.K2F[:], T.O8[:], T.SHI[:], A.add))
        vsync()
        wait("v", "gc", g_n)
        st["nj"] = []
        for j in range(8):
            sl = slice(128 * j, 128 * j + 128)
            vo(V.tensor_scalar(T.LL[:, sl], T.IOM[:], T.K1F[:, j:j + 1], None, A.is_equal))
            vo(V.tensor_scalar(T.RH[:, sl], T.ION[:], T.K2F[:, j:j + 1], T.HIF[:, j:j + 1], A.is_equal, A.mult))
            st["nj"].append(vo(V.tensor_scalar(T.RL[:, sl], T.ION[:], T.K2F[:, j:j + 1], T.LOF[:, j:j + 1], A.is_equal, A.mult)))

    def offsets():
        for j in range(8):
            sl = slice(128 * j, 128 * j + 128)
            wait("p", "v", st["nj"][j])
            P.matmul(T.PSO[:, 0:128], T.LL[:, sl], T.RH[:, sl], j == 0, False)
            ins = P.matmul(T.PSO[:, 0:128], T.LL[:, sl], T.RL[:, sl], False, j == 7)
        po = inc(ins, "p")
        wait("v", "p", po)
        st["noff"] = vo(V.tensor_copy(T.OFFALL[:], T.PSO[:, 0:128]))
        wait("g", "v", st["noff"])
        hp = HP[rk][c]
        rid, pid = topo.addr(hp, core)
        r0 = T.rank_of(RK[dg][0])
        g.remote_dma(T.REQH[:, rank * 32:rank * 32 + 32], T.OFFALL[:, r0 * 8:r0 * 8 + 32], T.sem.rqh, T.sem.ls, pid, rid,
                     _or(offE))
        cnt["ls"] = cnt.get("ls", 0) + len(offE)
        trs = []
        for hx, sem, e0 in ((rk, "rqr", 0), (cb, "rqc", 4)):
            r0 = T.rank_of(RK[hx][0])
            for i, d in enumerate(RK[hx]):
                trs.append(_tr(T, topo, core, d, offE[e0 + i], sem, T.OFFALL[:, r0 * 8:r0 * 8 + 32],
                               T.REQH[:, rank * 32:rank * 32 + 32]))
                cnt["ls"] += 1
        r0 = T.rank_of(RK[h][0])
        for i, d in enumerate(x for x in RK[h] if x != core):
            trs.append(_tr(T, topo, core, d, onE[2 * i] | onE[2 * i + 1], "rqo", T.OFFALL[:, r0 * 8:r0 * 8 + 32],
                           T.REQH[:, rank * 32:rank * 32 + 32]))
            cnt["ls"] += 2
        g.remote_dma_fused(trs, local_sem=T.sem.ls)
        vo(V.tensor_scalar(T.JLI[:], T.SI[:], 15, None, A.bitwise_and))
        vo(V.tensor_scalar(T.BI[:], T.SI[:], 4, 1, A.logical_shift_right, A.bitwise_and))
        vo(V.tensor_scalar(T.V1[:], T.SHI[:], 16.0, None, A.mult))
        vsync()
        vo(V.tensor_scalar(T.XB[:], T.BI[:], T.PAR[:, 0:1], 2048.0, A.not_equal, A.mult))
        vo(V.tensor_tensor(T.V2[:], T.V1[:], T.JLI[:], A.add))
        vsync()
        vo(V.tensor_tensor(T.V3[:], T.V2[:], T.O128[:], A.add))
        vsync()
        st["nval"] = vo(V.tensor_tensor(T.VAL[:], T.V3[:], T.XB[:], A.add))

    def cp(e, out, in_):
        if e == "v":
            return inc(V.tensor_copy(out, in_), "v")
        return inc(S.activation(out, in_, COPY), "a")

    wait("p", "gc", g_id)
    for w in range(NW):
        if w % 2 == 0:
            wait("p", "ld%d" % (w // 2), 16)
        if w >= 5:
            wait("p", evd[w - 5][0], evd[w - 5][1])
        pt = T["PT%d" % (w % 5)]
        for x in (0, 1):
            u = 2 * w + x
            ins = P.transpose(pt[:, 128 * x:128 * x + 128], T.A[:, 128 * u:128 * u + 128], T.IDENT[:])
        pun[w] = inc(ins, "p")
        e = "v" if (w >= 9 and w % 2 == 1) else "a"
        wait(e, "p", pun[w])
        lo, hi = slice(256 * w, 256 * w + 256), slice(4096 + 256 * w, 4096 + 256 * w + 256)
        cp(e, T.TT[0:64, lo], pt[0:64, 0:256])
        cp(e, T.TT[64:128, lo], pt[0:64, 0:256])
        cp(e, T.TT[64:128, hi], pt[64:128, 0:256])
        evd[w] = (e, cp(e, T.TT[0:64, hi], pt[64:128, 0:256]))
        if w == 1:
            prefix()
        if w == 5:
            offsets()
    ttv, tta = cnt["v"], cnt["a"]
    wait("p", "v", st["nval"])
    wait("p", "gc", g_lc)
    for k in range(4):
        ins = P.matmul(T.PSF[:, 8 * k:8 * k + 8], T.LC[:, 128 * k:128 * k + 128], T.VAL[:], True, True)
    pf = inc(ins, "p")

    for e in ("v", "a"):
        wait(e, "v", ttv)
        wait(e, "a", tta)
        wait(e, "tb", (len(onE) + len(offE)) * len(_handed()))
    done = {}
    for hx, sem, tot in ((dg, "rqd", 8), (cb, "rqc", 4), (rk, "rqr", 4), (h, "rqo", 6)):
        for i, qc in enumerate(RK[hx]):
            e = "v" if i < 2 else "a"
            wait(e, sem, tot)
            q = T.rank_of(qc)
            if qc == core:
                cp(e, T.LF[:, q * 128:q * 128 + 128], T.TT[:, 0:8192].indirect(T.OFFALL[:, 8 * q:8 * q + 8]))
            else:
                cp(e, T.G[:, q * 128:q * 128 + 128], T.TT[:, 0:8192].indirect(T.REQH[:, 32 * q + 8 * c:32 * q + 8 * c + 8]))
        done[hx] = (cnt["v"], cnt["a"])

    def gwait(hx):
        wait("g", "v", done[hx][0])
        wait("g", "a", done[hx][1])

    def piece(qc):
        q = T.rank_of(qc)
        return T.G[:, q * 128:q * 128 + 128]

    mine = T.LF[:, rank * 128:rank * 128 + 128]
    gwait(dg)
    trs = []
    for i, qc in enumerate(RK[dg]):
        hp, sem = (HP[rk][c], "rlS") if i < 2 else (HP[cb][c], "rlC")
        trs.append(_tr(T, topo, core, hp, offE[2 * i] | offE[2 * i + 1], sem, piece(qc), T.G[:, i * 128:i * 128 + 128]))
        cnt["ls"] += 2
    g.remote_dma_fused(trs, local_sem=T.sem.ls)
    gwait(cb)
    gwait(rk)
    trs = []
    for hx, sem, e0 in ((rk, "dtr", 0), (cb, "dtc", 4)):
        for i, qc in enumerate(RK[hx]):
            trs.append(_tr(T, topo, core, qc, offE[e0 + i], sem, piece(qc), mine))
            cnt["ls"] += 1
    g.remote_dma_fused(trs, local_sem=T.sem.ls)
    gwait(h)
    trs = []
    for i, qc in enumerate(x for x in RK[h] if x != core):
        trs.append(_tr(T, topo, core, qc, onE[2 * i] | onE[2 * i + 1], "dto", piece(qc), mine))
        cnt["ls"] += 2
    g.remote_dma_fused(trs, local_sem=T.sem.ls)

    wait("v", "p", pf)
    n_fo = vo(V.tensor_copy(T.FOFF[:], T.PSF[:, 0:32]))
    for hx, sem, tot in ((h, "dto", 6), (rk, "dtr", 4), (cb, "dtc", 4), (dg, "dtd", 8)):
        c0 = T.rank_of(RK[hx][0]) * 128
        for e in ("v", "a"):
            wait(e, sem, tot)
            if hx == h:
                wait(e, "v", done[h][0])
                wait(e, "a", done[h][1])
        cp("v", T.LF[64:128, 2048 + c0:2048 + c0 + 512], T.LF[0:64, c0:c0 + 512])
        cp("a", T.LF[0:64, 2048 + c0:2048 + c0 + 512], T.LF[64:128, c0:c0 + 512])
    cv, ca = cnt["v"], cnt["a"]
    gd = {}
    for e in ("v", "a"):
        wait(e, "v", cv)
        wait(e, "a", ca)
    for k in range(4):
        e = "v" if k % 2 == 0 else "a"
        gd[k] = (e, cp(e, T.YT[:, 128 * k:128 * k + 128], T.LF[:, 0:4096].indirect(T.FOFF[:, 8 * k:8 * k + 8])))
    wait("p", "v", cv)
    wait("p", "a", ca)
    for k in range(4):
        e = gd[k][0]
        wait("p", e, gd[k][1])
        pk = inc(P.transpose(T["PT%d" % k][:, 0:128], T.YT[:, 128 * k:128 * k + 128], T.IDENT[:]), "p")
        wait(e, "p", pk)
        cp(e, T.YS[:, 128 * k:128 * k + 128], T["PT%d" % k][:, 0:128])
    wait("q", "v", cnt["v"])
    wait("q", "a", cnt["a"])
    inc(Q.dma_start(T.y[:, :], T.YS[:]), "yst", 16)
    for name in sorted(cnt):
        if name != "yst":
            wait("g", name, cnt[name])
    wait("g", "yst", 16)
